import numpy as np
import ml_dtypes


def mxq(x, axis, fmt="e4m3"):
    dtype, down = {"e4m3": (ml_dtypes.float8_e4m3fn, 7), "e5m2": (ml_dtypes.float8_e5m2, 14)}[fmt]
    v = np.moveaxis(np.asarray(x, np.float32).astype(ml_dtypes.bfloat16).astype(np.float64), axis, -1)
    blocks = v.reshape(v.shape[:-1] + (-1, 32))
    amax = np.abs(blocks).max(-1, keepdims=True)
    byte = np.maximum(np.where(amax > 0, np.frexp(amax)[1] - 1 + 127, 0) - down, 1)
    scale = np.exp2(byte - 127.0)
    codes = (blocks / scale).astype(np.float32).astype(dtype).astype(np.float64)
    return np.moveaxis((codes * scale).reshape(v.shape), -1, axis)


WIDE = False


def mx_kscale(k):
    if not WIDE:
        return np.ones(k)
    levels = np.array([10, -10, 5, -5, 0])
    if k % 512:
        return np.exp2(np.random.permutation(np.resize(levels, k // 32))).repeat(32)
    a = np.empty((k // 512, 16))
    for p in range(k // 512):
        a[p, :8] = np.random.permutation(np.resize(levels, 8))
        for g in range(8):
            far = levels[np.abs(levels - a[p, g]) >= 10]
            a[p, g + 8] = far[np.random.randint(len(far))]
    return np.exp2(a.ravel()).repeat(32)


def f64(x):
    return np.asarray(x).astype(np.float64)


def striped(idx):
    return np.tile(idx.reshape(-1, 16).T, (8, 1)).astype(np.uint16)


def unstriped(offs):
    return offs[:16].T.reshape(-1).astype(np.int64)


E2M1 = np.array([0.0, 0.5, 1.0, 1.5, 2.0, 3.0, 4.0, 6.0, -0.0, -0.5, -1.0, -1.5, -2.0, -3.0, -4.0, -6.0])


def pack_fp4(w):
    k, n = w.shape
    w = f64(np.asarray(w, np.float32).astype(ml_dtypes.bfloat16)).reshape(k // 32, 32, n)
    amax = np.abs(w).max(1)
    mant, ex = np.frexp(amax / 6.0)
    byte = np.clip(np.where(amax > 0, np.where(mant > 0.5, ex, ex - 1) + 127, 1), 1, 254)
    scaled = (w * np.exp2(127.0 - byte)[:, None, :]).reshape(k, n).astype(np.float32)
    c = np.ascontiguousarray(scaled.reshape(k // 512, 128, 4, n).transpose(0, 1, 3, 2)).astype(ml_dtypes.float4_e2m1fn).view(np.uint8) & 0xF
    words = (c[..., 0::2] | (c[..., 1::2] << 4)).reshape(k // 512, 128, 2 * n)
    return np.ascontiguousarray(words), np.ascontiguousarray(byte.astype(np.uint8).reshape(k // 512, 16, n))


def unpack_fp4(words, scales):
    g, _, n = scales.shape
    words = np.ascontiguousarray(words).reshape(g, 128, n, 2)
    nib = np.empty((g, 128, n, 4), np.uint8)
    nib[..., 0::2] = words & 0xF
    nib[..., 1::2] = words >> 4
    vals = E2M1[nib] * np.repeat(np.exp2(scales.astype(np.float64) - 127.0), 8, axis=1)[..., None]
    return vals.transpose(0, 1, 3, 2).reshape(g * 512, n)


def relu(v):
    return np.maximum(v, 0.0)


K, T, H, N = 1024, 1024, 512, 256


def setup_inputs():
    n = np.random.standard_normal
    s = mx_kscale(K)[:, None]
    u = mx_kscale(H)
    packed_xT = pack_fp4(n((K, T)) * s)
    return {
        "x_words": packed_xT[0],
        "x_scales": packed_xT[1],
        "w1": (n((K, H)) / np.sqrt(K) / s * u).astype(np.float32),
        "w2": (n((H, N)) / np.sqrt(2 * H) / u[:, None]).astype(np.float32),
        "w3": (n((H, N)) / np.sqrt(2 * H) / u[:, None]).astype(np.float32),
        "pos1": striped(np.random.permutation(T)),
        "pos2": striped(np.random.permutation(T)),
        "pos3": striped(np.random.permutation(T)),
        "pos4": striped(np.random.permutation(T)),
    }


def reference(x_words, x_scales, w1, w2, w3, pos1, pos2, pos3, pos4):
    xq = unpack_fp4(x_words, x_scales)
    h = relu(mxq(f64(w1), 0, "e4m3").T @ xq)
    z = np.maximum(np.maximum(np.maximum(h[:, unstriped(pos1)], h[:, unstriped(pos2)]), h[:, unstriped(pos3)]), h[:, unstriped(pos4)])
    return relu(mxq(f64(w2), 0, "e4m3").T @ mxq(h, 0, "e4m3") + mxq(f64(w3), 0, "e4m3").T @ mxq(z, 0, "e4m3"))

@@ -1,0 +1,241 @@
+from contextlib import ExitStack
+
+import concourse.mybir as mybir
+
+K, T, H, N = 1024, 1024, 512, 256
+FLOPS = 2 * K * H * T + 2 * 2 * H * N * T
+
+F32 = mybir.dt.float32
+BF16 = mybir.dt.bfloat16
+I32 = mybir.dt.int32
+U32 = mybir.dt.uint32
+U16 = mybir.dt.uint16
+U8 = mybir.dt.uint8
+FP8X4 = mybir.dt.float8_e4m3fn_x4
+FP4X4 = mybir.dt.float4_e2m1fn_x4
+MAX = mybir.AluOpType.max
+RELU = mybir.ActivationFunctionType.Relu
+
+P = 128
+PACK = 4
+HALF = 512
+LISTS = 4
+
+
+def tile_picked_wsagecat_maxrelu_l_kernel(
+    tc, x_words, x_scales, w1, w2, w3, pos1, pos2, pos3, pos4, out
+):
+    nc = tc.nc
+    with ExitStack() as ctx:
+        held = ctx.enter_context(tc.tile_pool(name="held", bufs=1))
+        sb = ctx.enter_context(tc.tile_pool(name="sb", bufs=1))
+        psum = ctx.enter_context(tc.psum_pool(name="psum", bufs=1))
+
+        def tile(shape, dtype, name, tag=None):
+            return sb.tile(shape, dtype, name=name, tag=tag or name, align_bytes=64)
+
+        def bank(index, width, name):
+            return psum.tile([P, width], F32, name=name, tag="bank%d" % index)
+
+        xs = tile([P, 2, T], U8, "xs")
+        nc.gpsimd.memset(xs[:].bitcast(I32), 0)
+        w1_raw0 = tile([P, PACK, H], F32, "w1_raw0", "raw")
+        nc.sync.dma_start(out=w1_raw0[:], in_=w1[0:HALF, :].rearrange("(p j) c -> p j c", j=PACK))
+        for q in range(4):
+            nc.sync.dma_start(
+                out=xs[32 * q : 32 * q + 4, :, :].bitcast(I32),
+                in_=x_scales[:, 4 * q : 4 * q + 4, :].rearrange("z r c -> r z c").bitcast(I32),
+            )
+        xw = [tile([P, 2 * T], U8, "xw%d" % g) for g in range(2)]
+        nc.sync.dma_start(out=xw[0][:].bitcast(I32), in_=x_words[0].bitcast(I32))
+        w1_raw1 = []
+        for u in range(2):
+            raw = tile([P, PACK, H // 2], F32, "w1_raw1_%d" % u)
+            nc.sync.dma_start(
+                out=raw[:],
+                in_=w1[HALF:K, u * (H // 2) : (u + 1) * (H // 2)].rearrange("(p j) c -> p j c", j=PACK),
+            )
+            w1_raw1.append(raw)
+        nc.sync.dma_start(out=xw[1][:].bitcast(I32), in_=x_words[1].bitcast(I32))
+        lists = []
+        for d, pos in enumerate((pos1, pos2, pos3, pos4)):
+            offsets = held.tile([P, T // 16], U16, name="pos%d" % d)
+            nc.sync.dma_start(offsets[:], pos)
+            lists.append(offsets)
+
+        w1_codes = [tile([P, H], U32, "w1_codes%d" % g) for g in range(2)]
+        w1_scales = [tile([P, H], U8, "w1_scales%d" % g) for g in range(2)]
+        w1_bf = [tile([P, PACK * H], BF16, "w1_bf%d" % g) for g in range(2)]
+
+        def deal_w1(g, raw, m0, count):
+            dst = w1_bf[g][:].rearrange("p (t m j) -> p m j t", t=PACK, j=PACK)[:, m0 : m0 + count]
+            src = raw[:].rearrange("p j (m t) -> p m j t", t=PACK)
+            split = count * 5 // 8
+            nc.vector.tensor_copy(out=dst[:, 0:split], in_=src[:, 0:split])
+            nc.scalar.copy(out=dst[:, split:count], in_=src[:, split:count])
+
+        def quantize(codes, scales, values, c0, c1):
+            nc.vector.quantize_mx(
+                out=codes[:, c0:c1].bitcast(FP8X4), scales=scales[:, c0:c1], in_=values[:, PACK * c0 : PACK * c1]
+            )
+
+        deal_w1(0, w1_raw0, 0, P)
+        quantize(w1_codes[0], w1_scales[0], w1_bf[0], 0, 2 * P)
+        quantize(w1_codes[0], w1_scales[0], w1_bf[0], 2 * P, 4 * P)
+        deal_w1(1, w1_raw1[0], 0, P // 2)
+        deal_w1(1, w1_raw1[1], P // 2, P // 2)
+        quantize(w1_codes[1], w1_scales[1], w1_bf[1], 0, P)
+        quantize(w1_codes[1], w1_scales[1], w1_bf[1], P, 2 * P)
+        quantize(w1_codes[1], w1_scales[1], w1_bf[1], 2 * P, 4 * P)
+
+        w23_raw = tile([P, 2, PACK, N], F32, "w23_raw", "raw")
+        for e, w in enumerate((w2, w3)):
+            nc.sync.dma_start(out=w23_raw[:, e], in_=w.rearrange("(p j) n -> p j n", j=PACK))
+
+        h = [tile([P, T], F32, "h%d" % t) for t in range(PACK)]
+        h_bf = [tile([P, PACK, HALF], BF16, "h_bf%d" % c) for c in range(2)]
+        acc = {}
+        for t in range(PACK):
+            for c in range(2):
+                acc[t, c] = bank(2 * t + c, HALF, "acc%d_%d" % (t, c))
+            for g in range(2):
+                for c in range(2):
+                    nc.tensor.matmul_mx(
+                        out=acc[t, c][:],
+                        lhsT=w1_codes[g][:, t * P : (t + 1) * P].bitcast(FP8X4),
+                        lhsT_scale=w1_scales[g][:, t * P : (t + 1) * P],
+                        rhs=xw[g][:, 2 * c * HALF : 2 * (c + 1) * HALF].bitcast(FP4X4),
+                        rhs_scale=xs[:, g, c * HALF : (c + 1) * HALF],
+                        start=(g == 0),
+                        stop=(g == 1),
+                    )
+            nc.scalar.activation(h[t][:, 0:HALF], acc[t, 0][:], RELU)
+            if t == 0:
+                nc.vector.tensor_scalar_max(h[t][:, HALF:T], acc[t, 1][:], 0.0)
+            else:
+                nc.scalar.activation(h[t][:, HALF:T], acc[t, 1][:], RELU)
+
+        def weave(engine_copy, dst, src):
+            engine_copy(
+                out=dst.rearrange("p (c i t) -> p c t i", i=4, t=PACK),
+                in_=src.rearrange("p t (c i) -> p c t i", i=4),
+            )
+
+        w23_bf = tile([P, 2 * N * PACK], BF16, "w23_bf", "ring_w23")
+        for e in range(2):
+            weave(nc.scalar.copy, w23_bf[:, e * N * PACK : (e + 1) * N * PACK], w23_raw[:, e])
+        w23_codes = tile([P, 2 * N], U32, "w23_codes")
+        w23_scales = tile([P, 2 * N], U8, "w23_scales")
+
+        h_woven = []
+        for c in range(2):
+            for t in range(PACK):
+                nc.scalar.activation(h_bf[c][:, t, :], acc[t, c][:], RELU)
+            woven = tile([P, PACK * HALF], BF16, "h_woven%d" % c, "ring_h%d" % c)
+            weave(nc.scalar.copy, woven[:], h_bf[c][:])
+            h_woven.append(woven)
+        h_codes = tile([P, T], U32, "h_codes")
+        h_scales = tile([P, T], U8, "h_scales")
+
+        z = [tile([P, PACK, HALF], BF16, "z%d" % c) for c in range(2)]
+
+        def gather(dst, t, d, v0, v1):
+            nc.vector.tensor_copy(dst, h[t][:].indirect(lists[d][:, v0 // 16 : v1 // 16]))
+
+        def neighbours(t, v0, v1, tag=None):
+            n = v1 - v0
+            name = "%d_%d" % (t, v0)
+            got = tile([P, LISTS, n], BF16, "got" + name, tag)
+            for d in range(LISTS):
+                gather(got[:, d, :], t, d, v0, v1)
+            pair = tile([P, 2, n], BF16, "pair" + name)
+            nc.vector.tensor_tensor(pair[:], got[:, 0:2, :], got[:, 2:4, :], MAX)
+            c = v0 // HALF
+            nc.vector.tensor_tensor(z[c][:, t, v0 - c * HALF : v1 - c * HALF], pair[:, 0, :], pair[:, 1, :], MAX)
+
+        chunks = ((0, 512), (512, 768), (768, 896), (896, 1024))
+        res = {}
+
+        def product(index, m, e, codes, scales):
+            v0, v1 = chunks[index]
+            cols = slice(e * N + m * P, e * N + (m + 1) * P)
+            nc.tensor.matmul_mx(
+                out=res[index, m][:],
+                lhsT=w23_codes[:, cols].bitcast(FP8X4),
+                lhsT_scale=w23_scales[:, cols],
+                rhs=codes.bitcast(FP8X4),
+                rhs_scale=scales,
+                start=(e == 0),
+                stop=(e == 1),
+            )
+
+        def own_products(index):
+            v0, v1 = chunks[index]
+            for m in range(2):
+                res[index, m] = bank(2 * index + m, v1 - v0, "res%d_%d" % (index, m))
+                product(index, m, 0, h_codes[:, v0:v1], h_scales[:, v0:v1])
+
+        def weave_z(index, engine_copy):
+            v0, v1 = chunks[index]
+            c = v0 // HALF
+            woven = tile([P, PACK * (v1 - v0)], BF16, "z_woven%d" % index, "ring_z%d" % index)
+            weave(engine_copy, woven[:], z[c][:, :, v0 - c * HALF : v1 - c * HALF])
+            return woven
+
+        def finish(index, woven):
+            v0, v1 = chunks[index]
+            n = v1 - v0
+            codes = tile([P, n], U32, "z_codes%d" % index)
+            scales = tile([P, n], U8, "z_scales%d" % index)
+            quantize(codes, scales, woven, 0, n)
+            for m in range(2):
+                product(index, m, 1, codes[:], scales[:])
+            for m in range(2):
+                result = tile([P, n], F32, "result%d_%d" % (index, m), "ring_z1" if (index, m) == (0, 1) else None)
+                if index == 3 and m == 1:
+                    nc.vector.tensor_scalar_max(result[:], res[index, m][:], 0.0)
+                    nc.sync.dma_start(out=out[m * P : (m + 1) * P, v0:v1], in_=result[:])
+                elif index == 3:
+                    nc.scalar.activation(result[:], res[index, m][:], RELU)
+                    nc.scalar.dma_start(out=out[m * P : (m + 1) * P, v0:v1], in_=result[:])
+                else:
+                    nc.scalar.activation(result[:], res[index, m][:], RELU)
+                    nc.sync.dma_start(out=out[m * P : (m + 1) * P, v0:v1], in_=result[:])
+
+        neighbours(0, 0, HALF)
+        neighbours(0, HALF, T)
+        neighbours(1, 0, HALF)
+        quantize(w23_codes, w23_scales, w23_bf, 0, 2 * N)
+        neighbours(2, 0, HALF, "ring_w23")
+        quantize(h_codes[:, 0:HALF], h_scales[:, 0:HALF], h_woven[0], 0, HALF)
+        own_products(0)
+        neighbours(3, 0, HALF, "ring_h0")
+        woven0 = weave_z(0, nc.scalar.copy)
+        quantize(h_codes[:, HALF:T], h_scales[:, HALF:T], h_woven[1], 0, HALF)
+        for index in range(1, 4):
+            own_products(index)
+        neighbours(1, HALF, T, "ring_h1")
+        finish(0, woven0)
+        neighbours(2, HALF, T, "ring_z0")
+        neighbours(3, 512, 768)
+        woven1 = weave_z(1, nc.scalar.copy)
+        neighbours(3, 768, 896)
+        woven2 = weave_z(2, nc.scalar.copy)
+
+        v0, v1 = chunks[3]
+        n = v1 - v0
+        first = tile([P, 2, n], BF16, "last_first")
+        gather(first[:, 0, :], 3, 0, v0, v1)
+        gather(first[:, 1, :], 3, 1, v0, v1)
+        finish(1, woven1)
+        third = tile([P, n], BF16, "last_third", "ring_z1")
+        gather(third[:], 3, 2, v0, v1)
+        two = tile([P, n], BF16, "last_two")
+        nc.vector.tensor_tensor(two[:], first[:, 0, :], first[:, 1, :], MAX)
+        finish(2, woven2)
+        three = tile([P, n], BF16, "last_three")
+        nc.vector.tensor_tensor(three[:], two[:], third[:], MAX)
+        fourth = tile([P, n], BF16, "last_fourth", "ring_z2")
+        gather(fourth[:], 3, 3, v0, v1)
+        nc.vector.tensor_tensor(z[1][:, 3, v0 - HALF : v1 - HALF], three[:], fourth[:], MAX)
+        finish(3, weave_z(3, nc.vector.tensor_copy))

@@ -31,16 +31,27 @@ def tile_picked_wsagecat_maxrelu_l_kernel(
         sb = ctx.enter_context(tc.tile_pool(name="sb", bufs=1))
         psum = ctx.enter_context(tc.psum_pool(name="psum", bufs=1))
 
-        def tile(shape, dtype, name, tag=None):
-            return sb.tile(shape, dtype, name=name, tag=tag or name, align_bytes=64)
+        def tile(shape, dtype, name, tag=None, bufs=1):
+            return sb.tile(shape, dtype, name=name, tag=tag or name, align_bytes=64, bufs=bufs)
 
         def bank(index, width, name):
             return psum.tile([P, width], F32, name=name, tag="bank%d" % index)
 
         xs = tile([P, 2, T], U8, "xs")
         nc.gpsimd.memset(xs[:].bitcast(I32), 0)
-        w1_raw0 = tile([P, PACK, H], F32, "w1_raw0", "raw")
-        nc.sync.dma_start(out=w1_raw0[:], in_=w1[0:HALF, :].rearrange("(p j) c -> p j c", j=PACK))
+        w1_raw = {}
+
+        def load_w1(g, u):
+            w1_raw[g, u] = tile([P, PACK, H // 2], F32, "w1_raw%d_%d" % (g, u), "raw%d" % u if g == 0 else None)
+            nc.sync.dma_start(
+                out=w1_raw[g, u][:],
+                in_=w1[g * HALF : (g + 1) * HALF, u * (H // 2) : (u + 1) * (H // 2)].rearrange(
+                    "(p j) c -> p j c", j=PACK
+                ),
+            )
+
+        load_w1(0, 0)
+        load_w1(0, 1)
         for q in range(4):
             nc.sync.dma_start(
                 out=xs[32 * q : 32 * q + 4, :, :].bitcast(I32),
@@ -48,14 +59,8 @@ def tile_picked_wsagecat_maxrelu_l_kernel(
             )
         xw = [tile([P, 2 * T], U8, "xw%d" % g) for g in range(2)]
         nc.sync.dma_start(out=xw[0][:].bitcast(I32), in_=x_words[0].bitcast(I32))
-        w1_raw1 = []
-        for u in range(2):
-            raw = tile([P, PACK, H // 2], F32, "w1_raw1_%d" % u)
-            nc.sync.dma_start(
-                out=raw[:],
-                in_=w1[HALF:K, u * (H // 2) : (u + 1) * (H // 2)].rearrange("(p j) c -> p j c", j=PACK),
-            )
-            w1_raw1.append(raw)
+        load_w1(1, 0)
+        load_w1(1, 1)
         nc.sync.dma_start(out=xw[1][:].bitcast(I32), in_=x_words[1].bitcast(I32))
         lists = []
         for d, pos in enumerate((pos1, pos2, pos3, pos4)):
@@ -67,37 +72,47 @@ def tile_picked_wsagecat_maxrelu_l_kernel(
         w1_scales = [tile([P, H], U8, "w1_scales%d" % g) for g in range(2)]
         w1_bf = [tile([P, PACK * H], BF16, "w1_bf%d" % g) for g in range(2)]
 
-        def deal_w1(g, raw, m0, count):
-            dst = w1_bf[g][:].rearrange("p (t m j) -> p m j t", t=PACK, j=PACK)[:, m0 : m0 + count]
-            src = raw[:].rearrange("p j (m t) -> p m j t", t=PACK)
-            split = count * 5 // 8
-            nc.vector.tensor_copy(out=dst[:, 0:split], in_=src[:, 0:split])
-            nc.scalar.copy(out=dst[:, split:count], in_=src[:, split:count])
+        def deal_views(g, u):
+            dst = w1_bf[g][:].rearrange("p (t m j) -> p m j t", t=PACK, j=PACK)[:, u * (P // 2) : (u + 1) * (P // 2)]
+            src = w1_raw[g, u][:].rearrange("p j (m t) -> p m j t", t=PACK)
+            return dst, src
+
+        def deal_w1(g, u):
+            dst, src = deal_views(g, u)
+            nc.vector.tensor_copy(out=dst[:, 0:40], in_=src[:, 0:40])
+            nc.scalar.copy(out=dst[:, 40:64], in_=src[:, 40:64])
 
         def quantize(codes, scales, values, c0, c1):
             nc.vector.quantize_mx(
                 out=codes[:, c0:c1].bitcast(FP8X4), scales=scales[:, c0:c1], in_=values[:, PACK * c0 : PACK * c1]
             )
 
-        deal_w1(0, w1_raw0, 0, P)
-        quantize(w1_codes[0], w1_scales[0], w1_bf[0], 0, 2 * P)
+        deal_w1(0, 0)
+        deal_w1(0, 1)
+        quantize(w1_codes[0], w1_scales[0], w1_bf[0], 0, P)
+        quantize(w1_codes[0], w1_scales[0], w1_bf[0], P, 2 * P)
         quantize(w1_codes[0], w1_scales[0], w1_bf[0], 2 * P, 4 * P)
-        deal_w1(1, w1_raw1[0], 0, P // 2)
-        deal_w1(1, w1_raw1[1], P // 2, P // 2)
+        deal_w1(1, 0)
+        dst, src = deal_views(1, 1)
+        nc.vector.tensor_copy(out=dst[:, :, :, 0], in_=src[:, :, :, 0])
+        nc.scalar.copy(out=dst[:, :, :, 1:3], in_=src[:, :, :, 1:3])
         quantize(w1_codes[1], w1_scales[1], w1_bf[1], 0, P)
+        nc.vector.tensor_copy(out=dst[:, :, :, 3], in_=src[:, :, :, 3])
         quantize(w1_codes[1], w1_scales[1], w1_bf[1], P, 2 * P)
         quantize(w1_codes[1], w1_scales[1], w1_bf[1], 2 * P, 4 * P)
 
-        w23_raw = tile([P, 2, PACK, N], F32, "w23_raw", "raw")
+        w23_raw = []
         for e, w in enumerate((w2, w3)):
-            nc.sync.dma_start(out=w23_raw[:, e], in_=w.rearrange("(p j) n -> p j n", j=PACK))
+            raw = tile([P, PACK, N], F32, "w23_raw%d" % e, "raw%d" % e)
+            nc.sync.dma_start(out=raw[:], in_=w.rearrange("(p j) n -> p j n", j=PACK))
+            w23_raw.append(raw)
 
         h = [tile([P, T], F32, "h%d" % t) for t in range(PACK)]
-        h_bf = [tile([P, PACK, HALF], BF16, "h_bf%d" % c) for c in range(2)]
+        h_bf = tile([P, PACK, T], BF16, "h_bf")
         acc = {}
         for t in range(PACK):
             for c in range(2):
-                acc[t, c] = bank(2 * t + c, HALF, "acc%d_%d" % (t, c))
+                acc[t, c] = bank(2 * (t % 2) + c, HALF, "acc%d_%d" % (t, c))
             for g in range(2):
                 for c in range(2):
                     nc.tensor.matmul_mx(
@@ -123,16 +138,16 @@ def tile_picked_wsagecat_maxrelu_l_kernel(
 
         w23_bf = tile([P, 2 * N * PACK], BF16, "w23_bf", "ring_w23")
         for e in range(2):
-            weave(nc.scalar.copy, w23_bf[:, e * N * PACK : (e + 1) * N * PACK], w23_raw[:, e])
+            weave(nc.scalar.copy, w23_bf[:, e * N * PACK : (e + 1) * N * PACK], w23_raw[e][:])
         w23_codes = tile([P, 2 * N], U32, "w23_codes")
         w23_scales = tile([P, 2 * N], U8, "w23_scales")
 
         h_woven = []
+        for t in range(PACK):
+            nc.scalar.copy(h_bf[:, t, :], h[t][:])
         for c in range(2):
-            for t in range(PACK):
-                nc.scalar.activation(h_bf[c][:, t, :], acc[t, c][:], RELU)
             woven = tile([P, PACK * HALF], BF16, "h_woven%d" % c, "ring_h%d" % c)
-            weave(nc.scalar.copy, woven[:], h_bf[c][:])
+            weave(nc.scalar.copy, woven[:], h_bf[:, :, c * HALF : (c + 1) * HALF])
             h_woven.append(woven)
         h_codes = tile([P, T], U32, "h_codes")
         h_scales = tile([P, T], U8, "h_scales")
@@ -145,10 +160,10 @@ def tile_picked_wsagecat_maxrelu_l_kernel(
         def neighbours(t, v0, v1, tag=None):
             n = v1 - v0
             name = "%d_%d" % (t, v0)
-            got = tile([P, LISTS, n], BF16, "got" + name, tag)
+            got = tile([P, LISTS, n], BF16, "got" + name, "got", 2)
             for d in range(LISTS):
                 gather(got[:, d, :], t, d, v0, v1)
-            pair = tile([P, 2, n], BF16, "pair" + name)
+            pair = tile([P, 2, n], BF16, "pair" + name, tag)
             nc.vector.tensor_tensor(pair[:], got[:, 0:2, :], got[:, 2:4, :], MAX)
             c = v0 // HALF
             nc.vector.tensor_tensor(z[c][:, t, v0 - c * HALF : v1 - c * HALF], pair[:, 0, :], pair[:, 1, :], MAX)
@@ -172,7 +187,7 @@ def tile_picked_wsagecat_maxrelu_l_kernel(
         def own_products(index):
             v0, v1 = chunks[index]
             for m in range(2):
-                res[index, m] = bank(2 * index + m, v1 - v0, "res%d_%d" % (index, m))
+                res[index, m] = bank((4 + 2 * index + m) % 8, v1 - v0, "res%d_%d" % (index, m))
                 product(index, m, 0, h_codes[:, v0:v1], h_scales[:, v0:v1])
 
         def weave_z(index, engine_copy):
@@ -191,7 +206,7 @@ def tile_picked_wsagecat_maxrelu_l_kernel(
             for m in range(2):
                 product(index, m, 1, codes[:], scales[:])
             for m in range(2):
-                result = tile([P, n], F32, "result%d_%d" % (index, m), "ring_z1" if (index, m) == (0, 1) else None)
+                result = tile([P, n], F32, "result%d_%d" % (index, m))
                 if index == 3 and m == 1:
                     nc.vector.tensor_scalar_max(result[:], res[index, m][:], 0.0)
                     nc.sync.dma_start(out=out[m * P : (m + 1) * P, v0:v1], in_=result[:])
@@ -203,20 +218,19 @@ def tile_picked_wsagecat_maxrelu_l_kernel(
                     nc.sync.dma_start(out=out[m * P : (m + 1) * P, v0:v1], in_=result[:])
 
         neighbours(0, 0, HALF)
-        neighbours(0, HALF, T)
-        neighbours(1, 0, HALF)
         quantize(w23_codes, w23_scales, w23_bf, 0, 2 * N)
-        neighbours(2, 0, HALF, "ring_w23")
+        neighbours(0, HALF, T, "ring_w23")
         quantize(h_codes[:, 0:HALF], h_scales[:, 0:HALF], h_woven[0], 0, HALF)
         own_products(0)
-        neighbours(3, 0, HALF, "ring_h0")
-        woven0 = weave_z(0, nc.scalar.copy)
+        neighbours(1, 0, HALF, "ring_h0")
         quantize(h_codes[:, HALF:T], h_scales[:, HALF:T], h_woven[1], 0, HALF)
         for index in range(1, 4):
             own_products(index)
-        neighbours(1, HALF, T, "ring_h1")
-        finish(0, woven0)
-        neighbours(2, HALF, T, "ring_z0")
+        neighbours(2, 0, HALF, "ring_h1")
+        neighbours(3, 0, HALF)
+        finish(0, weave_z(0, nc.scalar.copy))
+        neighbours(1, HALF, T, "ring_z0")
+        neighbours(2, HALF, T)
         neighbours(3, 512, 768)
         woven1 = weave_z(1, nc.scalar.copy)
         neighbours(3, 768, 896)
@@ -224,7 +238,7 @@ def tile_picked_wsagecat_maxrelu_l_kernel(
 
         v0, v1 = chunks[3]
         n = v1 - v0
-        first = tile([P, 2, n], BF16, "last_first")
+        first = tile([P, 2, n], BF16, "last_first", "got", 2)
         gather(first[:, 0, :], 3, 0, v0, v1)
         gather(first[:, 1, :], 3, 1, v0, v1)
         finish(1, woven1)

@@ -108,7 +108,7 @@ def tile_picked_wsagecat_maxrelu_l_kernel(
             w23_raw.append(raw)
 
         h = [tile([P, T], F32, "h%d" % t) for t in range(PACK)]
-        h_bf = tile([P, PACK, T], BF16, "h_bf")
+        h_bf = [tile([P, PACK, HALF], BF16, "h_bf%d" % c) for c in range(2)]
         acc = {}
         for t in range(PACK):
             for c in range(2):
@@ -136,37 +136,32 @@ def tile_picked_wsagecat_maxrelu_l_kernel(
                 in_=src.rearrange("p t (c i) -> p c t i", i=4),
             )
 
-        w23_bf = tile([P, 2 * N * PACK], BF16, "w23_bf", "ring_w23")
+        w23_bf = tile([P, 2 * N * PACK], BF16, "w23_bf")
         for e in range(2):
             weave(nc.scalar.copy, w23_bf[:, e * N * PACK : (e + 1) * N * PACK], w23_raw[e][:])
         w23_codes = tile([P, 2 * N], U32, "w23_codes")
         w23_scales = tile([P, 2 * N], U8, "w23_scales")
 
         h_woven = []
-        for t in range(PACK):
-            nc.scalar.copy(h_bf[:, t, :], h[t][:])
         for c in range(2):
-            woven = tile([P, PACK * HALF], BF16, "h_woven%d" % c, "ring_h%d" % c)
-            weave(nc.scalar.copy, woven[:], h_bf[:, :, c * HALF : (c + 1) * HALF])
+            for t in range(PACK):
+                nc.scalar.copy(h_bf[c][:, t, :], h[t][:, c * HALF : (c + 1) * HALF])
+            woven = tile([P, PACK * HALF], BF16, "h_woven%d" % c)
+            weave(nc.scalar.copy, woven[:], h_bf[c][:])
             h_woven.append(woven)
         h_codes = tile([P, T], U32, "h_codes")
         h_scales = tile([P, T], U8, "h_scales")
 
-        z = [tile([P, PACK, HALF], BF16, "z%d" % c) for c in range(2)]
+        z_ranges = ((0, 512), (512, 768), (768, 1024))
+        z = [tile([P, PACK, v1 - v0], BF16, "z%d" % c) for c, (v0, v1) in enumerate(z_ranges)]
+
+        def z_parts(v0, v1):
+            return [
+                (z[c], max(v0, a), min(v1, b), a) for c, (a, b) in enumerate(z_ranges) if max(v0, a) < min(v1, b)
+            ]
 
         def gather(dst, t, d, v0, v1):
             nc.vector.tensor_copy(dst, h[t][:].indirect(lists[d][:, v0 // 16 : v1 // 16]))
-
-        def neighbours(t, v0, v1, tag=None):
-            n = v1 - v0
-            name = "%d_%d" % (t, v0)
-            got = tile([P, LISTS, n], BF16, "got" + name, "got", 2)
-            for d in range(LISTS):
-                gather(got[:, d, :], t, d, v0, v1)
-            pair = tile([P, 2, n], BF16, "pair" + name, tag)
-            nc.vector.tensor_tensor(pair[:], got[:, 0:2, :], got[:, 2:4, :], MAX)
-            c = v0 // HALF
-            nc.vector.tensor_tensor(z[c][:, t, v0 - c * HALF : v1 - c * HALF], pair[:, 0, :], pair[:, 1, :], MAX)
 
         chunks = ((0, 512), (512, 768), (768, 896), (896, 1024))
         res = {}
@@ -192,9 +187,9 @@ def tile_picked_wsagecat_maxrelu_l_kernel(
 
         def weave_z(index, engine_copy):
             v0, v1 = chunks[index]
-            c = v0 // HALF
-            woven = tile([P, PACK * (v1 - v0)], BF16, "z_woven%d" % index, "ring_z%d" % index)
-            weave(engine_copy, woven[:], z[c][:, :, v0 - c * HALF : v1 - c * HALF])
+            ((part, a, b, base),) = z_parts(v0, v1)
+            woven = tile([P, PACK * (v1 - v0)], BF16, "z_woven%d" % index)
+            weave(engine_copy, woven[:], part[:, :, a - base : b - base])
             return woven
 
         def finish(index, woven):
@@ -217,39 +212,74 @@ def tile_picked_wsagecat_maxrelu_l_kernel(
                     nc.scalar.activation(result[:], res[index, m][:], RELU)
                     nc.sync.dma_start(out=out[m * P : (m + 1) * P, v0:v1], in_=result[:])
 
-        neighbours(0, 0, HALF)
+        units = ((0, 0, 512), (0, 512, 1024), (1, 0, 512), (2, 0, 512), (3, 0, 512), (1, 512, 1024),
+                 (2, 512, 1024), (3, 512, 768), (3, 768, 896), (3, 896, 1024))
+        got = {}
+
+        def stage(first, last, tag):
+            widths = [2 * (units[k // 2][2] - units[k // 2][1]) for k in range(first, last)]
+            room = tile([P, sum(widths)], BF16, "got%d" % first, tag)
+            at = 0
+            for k, width in zip(range(first, last), widths):
+                got[k] = room[:, at : at + width]
+                at = at + width
+
+        def fetch(u, d):
+            t, v0, v1 = units[u]
+            n = v1 - v0
+            gather(got[2 * u + d // 2][:, (d % 2) * n : (d % 2 + 1) * n], t, d, v0, v1)
+
+        def step(u):
+            t, v0, v1 = units[u]
+            n = v1 - v0
+            fetch(u, 2)
+            fetch(u, 3)
+            fetch(u + 1, 0)
+            pair = tile([P, 2 * n], BF16, "pair%d" % u)
+            nc.vector.tensor_tensor(pair[:], got[2 * u], got[2 * u + 1], MAX)
+            fetch(u + 1, 1)
+            for part, a, b, base in z_parts(v0, v1):
+                nc.vector.tensor_tensor(
+                    part[:, t, a - base : b - base], pair[:, a - v0 : b - v0], pair[:, n + a - v0 : n + b - v0], MAX
+                )
+
+        stage(0, 5, None)
+        fetch(0, 0)
+        fetch(0, 1)
+        step(0)
+        step(1)
         quantize(w23_codes, w23_scales, w23_bf, 0, 2 * N)
-        neighbours(0, HALF, T, "ring_w23")
+        stage(5, 7, "raw1")
+        step(2)
         quantize(h_codes[:, 0:HALF], h_scales[:, 0:HALF], h_woven[0], 0, HALF)
         own_products(0)
-        neighbours(1, 0, HALF, "ring_h0")
+        stage(7, 9, "h_bf0")
+        step(3)
         quantize(h_codes[:, HALF:T], h_scales[:, HALF:T], h_woven[1], 0, HALF)
         for index in range(1, 4):
             own_products(index)
-        neighbours(2, 0, HALF, "ring_h1")
-        neighbours(3, 0, HALF)
-        finish(0, weave_z(0, nc.scalar.copy))
-        neighbours(1, HALF, T, "ring_z0")
-        neighbours(2, HALF, T)
-        neighbours(3, 512, 768)
+        stage(9, 13, "h_bf1")
+        step(4)
+        woven0 = weave_z(0, nc.scalar.copy)
+        step(5)
+        finish(0, woven0)
+        stage(13, 19, "z0")
+        step(6)
+        step(7)
         woven1 = weave_z(1, nc.scalar.copy)
-        neighbours(3, 768, 896)
+        step(8)
         woven2 = weave_z(2, nc.scalar.copy)
 
         v0, v1 = chunks[3]
         n = v1 - v0
-        first = tile([P, 2, n], BF16, "last_first", "got", 2)
-        gather(first[:, 0, :], 3, 0, v0, v1)
-        gather(first[:, 1, :], 3, 1, v0, v1)
-        finish(1, woven1)
-        third = tile([P, n], BF16, "last_third", "ring_z1")
-        gather(third[:], 3, 2, v0, v1)
         two = tile([P, n], BF16, "last_two")
-        nc.vector.tensor_tensor(two[:], first[:, 0, :], first[:, 1, :], MAX)
-        finish(2, woven2)
+        nc.vector.tensor_tensor(two[:], got[18][:, 0:n], got[18][:, n : 2 * n], MAX)
+        finish(1, woven1)
+        stage(19, 20, "z1")
+        fetch(9, 2)
+        fetch(9, 3)
         three = tile([P, n], BF16, "last_three")
-        nc.vector.tensor_tensor(three[:], two[:], third[:], MAX)
-        fourth = tile([P, n], BF16, "last_fourth", "ring_z2")
-        gather(fourth[:], 3, 3, v0, v1)
-        nc.vector.tensor_tensor(z[1][:, 3, v0 - HALF : v1 - HALF], three[:], fourth[:], MAX)
+        nc.vector.tensor_tensor(three[:], two[:], got[19][:, 0:n], MAX)
+        finish(2, woven2)
+        nc.vector.tensor_tensor(z[2][:, 3, n : 2 * n], three[:], got[19][:, n : 2 * n], MAX)
         finish(3, weave_z(3, nc.vector.tensor_copy))

@@ -18,8 +18,20 @@ RELU = mybir.ActivationFunctionType.Relu
 
 P = 128
 PACK = 4
-HALF = 512
+K_PASS = P * PACK
+BANK = 512
+BANKS = 8
 LISTS = 4
+ENTRIES = 16
+RUN = 4
+
+VECTOR_DEALS = 80
+
+CHUNKS = ((0, 512), (512, 768), (768, 896), (896, 1024))
+LAST = len(CHUNKS) - 1
+Z_TILES = ((0, 512), (512, 768), (768, 1024))
+UNITS = ((0, 0, T), (1, 0, T), (2, 0, 512), (3, 0, 512), (2, 512, T)) + tuple((3, a, b) for a, b in CHUNKS[1:])
+WHOLE_PLANES = 2
 
 
 def tile_picked_wsagecat_maxrelu_l_kernel(
@@ -31,75 +43,80 @@ def tile_picked_wsagecat_maxrelu_l_kernel(
         sb = ctx.enter_context(tc.tile_pool(name="sb", bufs=1))
         psum = ctx.enter_context(tc.psum_pool(name="psum", bufs=1))
 
-        def tile(shape, dtype, name, tag=None, bufs=1):
-            return sb.tile(shape, dtype, name=name, tag=tag or name, align_bytes=64, bufs=bufs)
+        def tile(shape, dtype, name, tag=None):
+            return sb.tile(shape, dtype, name=name, tag=tag or name, align_bytes=64)
 
-        def bank(index, width, name):
-            return psum.tile([P, width], F32, name=name, tag="bank%d" % index)
+        def bank(number, width, name):
+            return psum.tile([P, width], F32, name=name, tag="bank%d" % number)
 
-        xs = tile([P, 2, T], U8, "xs")
-        nc.gpsimd.memset(xs[:].bitcast(I32), 0)
+        def quantize(codes, scales, values):
+            nc.vector.quantize_mx(out=codes.bitcast(FP8X4), scales=scales, in_=values)
+
+        def weave(copy, dst, planes):
+            copy(
+                out=dst.rearrange("p (c i t) -> p c t i", i=RUN, t=PACK),
+                in_=planes.rearrange("p t (c i) -> p c t i", i=RUN),
+            )
+
+        x_scale = tile([P, 2, T], U8, "x_scale")
+        nc.gpsimd.memset(x_scale[:].bitcast(I32), 0)
+
         w1_raw = {}
 
         def load_w1(g, u):
-            w1_raw[g, u] = tile([P, PACK, H // 2], F32, "w1_raw%d_%d" % (g, u), "raw%d" % u if g == 0 else None)
-            nc.sync.dma_start(
-                out=w1_raw[g, u][:],
-                in_=w1[g * HALF : (g + 1) * HALF, u * (H // 2) : (u + 1) * (H // 2)].rearrange(
-                    "(p j) c -> p j c", j=PACK
-                ),
-            )
+            w1_raw[g, u] = tile([P, 2, H], F32, "w1_raw%d_%d" % (g, u), "raw%d" % u if g == 0 else None)
+            rows = w1[g * K_PASS : (g + 1) * K_PASS, :].rearrange("(p j) c -> p j c", j=PACK)
+            nc.sync.dma_start(out=w1_raw[g, u][:], in_=rows[:, 2 * u : 2 * u + 2, :])
 
         load_w1(0, 0)
         load_w1(0, 1)
         for q in range(4):
             nc.sync.dma_start(
-                out=xs[32 * q : 32 * q + 4, :, :].bitcast(I32),
-                in_=x_scales[:, 4 * q : 4 * q + 4, :].rearrange("z r c -> r z c").bitcast(I32),
+                out=x_scale[32 * q : 32 * q + 4, :, :].bitcast(I32),
+                in_=x_scales[:, 4 * q : 4 * q + 4, :].rearrange("g r c -> r g c").bitcast(I32),
             )
-        xw = [tile([P, 2 * T], U8, "xw%d" % g) for g in range(2)]
-        nc.sync.dma_start(out=xw[0][:].bitcast(I32), in_=x_words[0].bitcast(I32))
+        x_code = [tile([P, 2 * T], U8, "x_code%d" % g) for g in range(2)]
+        nc.sync.dma_start(out=x_code[0][:].bitcast(I32), in_=x_words[0].bitcast(I32))
         load_w1(1, 0)
         load_w1(1, 1)
-        nc.sync.dma_start(out=xw[1][:].bitcast(I32), in_=x_words[1].bitcast(I32))
+        nc.sync.dma_start(out=x_code[1][:].bitcast(I32), in_=x_words[1].bitcast(I32))
         lists = []
         for d, pos in enumerate((pos1, pos2, pos3, pos4)):
-            offsets = held.tile([P, T // 16], U16, name="pos%d" % d)
+            offsets = held.tile([P, T // ENTRIES], U16, name="list%d" % d)
             nc.sync.dma_start(offsets[:], pos)
             lists.append(offsets)
 
-        w1_codes = [tile([P, H], U32, "w1_codes%d" % g) for g in range(2)]
-        w1_scales = [tile([P, H], U8, "w1_scales%d" % g) for g in range(2)]
-        w1_bf = [tile([P, PACK * H], BF16, "w1_bf%d" % g) for g in range(2)]
+        w1_code = [tile([P, H], U32, "w1_code%d" % g) for g in range(2)]
+        w1_scale = [tile([P, H], U8, "w1_scale%d" % g) for g in range(2)]
+        w1_dealt = [tile([P, PACK * H], BF16, "w1_dealt%d" % g) for g in range(2)]
 
         def deal_views(g, u):
-            dst = w1_bf[g][:].rearrange("p (t m j) -> p m j t", t=PACK, j=PACK)[:, u * (P // 2) : (u + 1) * (P // 2)]
+            dst = w1_dealt[g][:].rearrange("p (t m j) -> p m j t", t=PACK, j=PACK)[:, :, 2 * u : 2 * u + 2]
             src = w1_raw[g, u][:].rearrange("p j (m t) -> p m j t", t=PACK)
             return dst, src
 
-        def deal_w1(g, u):
+        def deal(g, u):
             dst, src = deal_views(g, u)
-            nc.vector.tensor_copy(out=dst[:, 0:40], in_=src[:, 0:40])
-            nc.scalar.copy(out=dst[:, 40:64], in_=src[:, 40:64])
+            nc.vector.tensor_copy(out=dst[:, 0:VECTOR_DEALS], in_=src[:, 0:VECTOR_DEALS])
+            nc.scalar.copy(out=dst[:, VECTOR_DEALS:P], in_=src[:, VECTOR_DEALS:P])
 
-        def quantize(codes, scales, values, c0, c1):
-            nc.vector.quantize_mx(
-                out=codes[:, c0:c1].bitcast(FP8X4), scales=scales[:, c0:c1], in_=values[:, PACK * c0 : PACK * c1]
-            )
+        def quantize_w1(g, t0, t1):
+            cols = slice(t0 * P, t1 * P)
+            quantize(w1_code[g][:, cols], w1_scale[g][:, cols], w1_dealt[g][:, t0 * K_PASS : t1 * K_PASS])
 
-        deal_w1(0, 0)
-        deal_w1(0, 1)
-        quantize(w1_codes[0], w1_scales[0], w1_bf[0], 0, P)
-        quantize(w1_codes[0], w1_scales[0], w1_bf[0], P, 2 * P)
-        quantize(w1_codes[0], w1_scales[0], w1_bf[0], 2 * P, 4 * P)
-        deal_w1(1, 0)
+        deal(0, 0)
+        deal(0, 1)
+        quantize_w1(0, 0, 1)
+        quantize_w1(0, 1, 2)
+        quantize_w1(0, 2, 4)
+        deal(1, 0)
         dst, src = deal_views(1, 1)
         nc.vector.tensor_copy(out=dst[:, :, :, 0], in_=src[:, :, :, 0])
         nc.scalar.copy(out=dst[:, :, :, 1:3], in_=src[:, :, :, 1:3])
-        quantize(w1_codes[1], w1_scales[1], w1_bf[1], 0, P)
+        quantize_w1(1, 0, 1)
         nc.vector.tensor_copy(out=dst[:, :, :, 3], in_=src[:, :, :, 3])
-        quantize(w1_codes[1], w1_scales[1], w1_bf[1], P, 2 * P)
-        quantize(w1_codes[1], w1_scales[1], w1_bf[1], 2 * P, 4 * P)
+        quantize_w1(1, 1, 2)
+        quantize_w1(1, 2, 4)
 
         w23_raw = []
         for e, w in enumerate((w2, w3)):
@@ -107,179 +124,171 @@ def tile_picked_wsagecat_maxrelu_l_kernel(
             nc.sync.dma_start(out=raw[:], in_=w.rearrange("(p j) n -> p j n", j=PACK))
             w23_raw.append(raw)
 
-        h = [tile([P, T], F32, "h%d" % t) for t in range(PACK)]
-        h_bf = [tile([P, PACK, HALF], BF16, "h_bf%d" % c) for c in range(2)]
-        acc = {}
+        h = [tile([P, 2 * T if t < WHOLE_PLANES else T], F32, "h%d" % t) for t in range(PACK)]
         for t in range(PACK):
-            for c in range(2):
-                acc[t, c] = bank(2 * (t % 2) + c, HALF, "acc%d_%d" % (t, c))
+            acc = [bank(2 * (t % 2) + c, BANK, "acc%d_%d" % (t, c)) for c in range(2)]
             for g in range(2):
                 for c in range(2):
                     nc.tensor.matmul_mx(
-                        out=acc[t, c][:],
-                        lhsT=w1_codes[g][:, t * P : (t + 1) * P].bitcast(FP8X4),
-                        lhsT_scale=w1_scales[g][:, t * P : (t + 1) * P],
-                        rhs=xw[g][:, 2 * c * HALF : 2 * (c + 1) * HALF].bitcast(FP4X4),
-                        rhs_scale=xs[:, g, c * HALF : (c + 1) * HALF],
+                        out=acc[c][:],
+                        lhsT=w1_code[g][:, t * P : (t + 1) * P].bitcast(FP8X4),
+                        lhsT_scale=w1_scale[g][:, t * P : (t + 1) * P],
+                        rhs=x_code[g][:, 2 * c * BANK : 2 * (c + 1) * BANK].bitcast(FP4X4),
+                        rhs_scale=x_scale[:, g, c * BANK : (c + 1) * BANK],
                         start=(g == 0),
                         stop=(g == 1),
                     )
-            nc.scalar.activation(h[t][:, 0:HALF], acc[t, 0][:], RELU)
+            nc.scalar.activation(h[t][:, 0:BANK], acc[0][:], RELU)
             if t == 0:
-                nc.vector.tensor_scalar_max(h[t][:, HALF:T], acc[t, 1][:], 0.0)
+                nc.vector.tensor_scalar_max(h[t][:, BANK:T], acc[1][:], 0.0)
             else:
-                nc.scalar.activation(h[t][:, HALF:T], acc[t, 1][:], RELU)
+                nc.scalar.activation(h[t][:, BANK:T], acc[1][:], RELU)
 
-        def weave(engine_copy, dst, src):
-            engine_copy(
-                out=dst.rearrange("p (c i t) -> p c t i", i=4, t=PACK),
-                in_=src.rearrange("p t (c i) -> p c t i", i=4),
-            )
-
-        w23_bf = tile([P, 2 * N * PACK], BF16, "w23_bf")
+        w23_woven = tile([P, 2 * N * PACK], BF16, "w23_woven")
         for e in range(2):
-            weave(nc.scalar.copy, w23_bf[:, e * N * PACK : (e + 1) * N * PACK], w23_raw[e][:])
-        w23_codes = tile([P, 2 * N], U32, "w23_codes")
-        w23_scales = tile([P, 2 * N], U8, "w23_scales")
+            weave(nc.scalar.copy, w23_woven[:, e * N * PACK : (e + 1) * N * PACK], w23_raw[e][:])
+        w23_code = tile([P, 2 * N], U32, "w23_code")
+        w23_scale = tile([P, 2 * N], U8, "w23_scale")
 
         h_woven = []
         for c in range(2):
+            planes = tile([P, PACK, BANK], BF16, "h_planes%d" % c)
             for t in range(PACK):
-                nc.scalar.copy(h_bf[c][:, t, :], h[t][:, c * HALF : (c + 1) * HALF])
-            woven = tile([P, PACK * HALF], BF16, "h_woven%d" % c)
-            weave(nc.scalar.copy, woven[:], h_bf[c][:])
+                nc.scalar.copy(planes[:, t, :], h[t][:, c * BANK : (c + 1) * BANK])
+            woven = tile([P, PACK * BANK], BF16, "h_woven%d" % c)
+            weave(nc.scalar.copy, woven[:], planes[:])
             h_woven.append(woven)
-        h_codes = tile([P, T], U32, "h_codes")
-        h_scales = tile([P, T], U8, "h_scales")
+        h_code = tile([P, T], U32, "h_code")
+        h_scale = tile([P, T], U8, "h_scale")
 
-        z_ranges = ((0, 512), (512, 768), (768, 1024))
-        z = [tile([P, PACK, v1 - v0], BF16, "z%d" % c) for c, (v0, v1) in enumerate(z_ranges)]
+        def quantize_h(c):
+            cols = slice(c * BANK, (c + 1) * BANK)
+            quantize(h_code[:, cols], h_scale[:, cols], h_woven[c][:])
 
-        def z_parts(v0, v1):
-            return [
-                (z[c], max(v0, a), min(v1, b), a) for c, (a, b) in enumerate(z_ranges) if max(v0, a) < min(v1, b)
-            ]
-
-        def gather(dst, t, d, v0, v1):
-            nc.vector.tensor_copy(dst, h[t][:].indirect(lists[d][:, v0 // 16 : v1 // 16]))
-
-        chunks = ((0, 512), (512, 768), (768, 896), (896, 1024))
+        z = [tile([P, PACK, b - a], BF16, "z%d" % c) for c, (a, b) in enumerate(Z_TILES)]
         res = {}
 
-        def product(index, m, e, codes, scales):
-            v0, v1 = chunks[index]
+        def z_parts(v0, v1):
+            return [(z[c], max(v0, a), min(v1, b), a) for c, (a, b) in enumerate(Z_TILES) if max(v0, a) < min(v1, b)]
+
+        def multiply(chunk, m, e, codes, scales):
             cols = slice(e * N + m * P, e * N + (m + 1) * P)
             nc.tensor.matmul_mx(
-                out=res[index, m][:],
-                lhsT=w23_codes[:, cols].bitcast(FP8X4),
-                lhsT_scale=w23_scales[:, cols],
+                out=res[chunk, m][:],
+                lhsT=w23_code[:, cols].bitcast(FP8X4),
+                lhsT_scale=w23_scale[:, cols],
                 rhs=codes.bitcast(FP8X4),
                 rhs_scale=scales,
                 start=(e == 0),
                 stop=(e == 1),
             )
 
-        def own_products(index):
-            v0, v1 = chunks[index]
+        def open_groups(chunk):
+            v0, v1 = CHUNKS[chunk]
             for m in range(2):
-                res[index, m] = bank((4 + 2 * index + m) % 8, v1 - v0, "res%d_%d" % (index, m))
-                product(index, m, 0, h_codes[:, v0:v1], h_scales[:, v0:v1])
+                res[chunk, m] = bank((4 + 2 * chunk + m) % BANKS, v1 - v0, "res%d_%d" % (chunk, m))
+                multiply(chunk, m, 0, h_code[:, v0:v1], h_scale[:, v0:v1])
 
-        def weave_z(index, engine_copy):
-            v0, v1 = chunks[index]
+        def weave_z(chunk, copy):
+            v0, v1 = CHUNKS[chunk]
             ((part, a, b, base),) = z_parts(v0, v1)
-            woven = tile([P, PACK * (v1 - v0)], BF16, "z_woven%d" % index)
-            weave(engine_copy, woven[:], part[:, :, a - base : b - base])
+            woven = tile([P, PACK * (v1 - v0)], BF16, "z_woven%d" % chunk)
+            weave(copy, woven[:], part[:, :, a - base : b - base])
             return woven
 
-        def finish(index, woven):
-            v0, v1 = chunks[index]
-            n = v1 - v0
-            codes = tile([P, n], U32, "z_codes%d" % index)
-            scales = tile([P, n], U8, "z_scales%d" % index)
-            quantize(codes, scales, woven, 0, n)
+        def close_groups(chunk, woven):
+            v0, v1 = CHUNKS[chunk]
+            codes = tile([P, v1 - v0], U32, "z_code%d" % chunk)
+            scales = tile([P, v1 - v0], U8, "z_scale%d" % chunk)
+            quantize(codes[:], scales[:], woven[:])
             for m in range(2):
-                product(index, m, 1, codes[:], scales[:])
-            for m in range(2):
-                result = tile([P, n], F32, "result%d_%d" % (index, m))
-                if index == 3 and m == 1:
-                    nc.vector.tensor_scalar_max(result[:], res[index, m][:], 0.0)
-                    nc.sync.dma_start(out=out[m * P : (m + 1) * P, v0:v1], in_=result[:])
-                elif index == 3:
-                    nc.scalar.activation(result[:], res[index, m][:], RELU)
-                    nc.scalar.dma_start(out=out[m * P : (m + 1) * P, v0:v1], in_=result[:])
-                else:
-                    nc.scalar.activation(result[:], res[index, m][:], RELU)
-                    nc.sync.dma_start(out=out[m * P : (m + 1) * P, v0:v1], in_=result[:])
+                multiply(chunk, m, 1, codes[:], scales[:])
 
-        units = ((0, 0, 512), (0, 512, 1024), (1, 0, 512), (2, 0, 512), (3, 0, 512), (1, 512, 1024),
-                 (2, 512, 1024), (3, 512, 768), (3, 768, 896), (3, 896, 1024))
-        got = {}
+        def store(chunk, m):
+            v0, v1 = CHUNKS[chunk]
+            result = tile([P, v1 - v0], F32, "result%d_%d" % (chunk, m))
+            if (chunk, m) == (LAST, 1):
+                nc.vector.tensor_scalar_max(result[:], res[chunk, m][:], 0.0)
+            else:
+                nc.scalar.activation(result[:], res[chunk, m][:], RELU)
+            queue = nc.scalar if (chunk, m) == (LAST, 0) else nc.sync
+            queue.dma_start(out=out[m * P : (m + 1) * P, v0:v1], in_=result[:])
 
-        def stage(first, last, tag):
-            widths = [2 * (units[k // 2][2] - units[k // 2][1]) for k in range(first, last)]
+        place = {}
+
+        def make_room(first, end, tag):
+            widths = [UNITS[k // LISTS][2] - UNITS[k // LISTS][1] for k in range(first, end)]
             room = tile([P, sum(widths)], BF16, "got%d" % first, tag)
-            at = 0
-            for k, width in zip(range(first, last), widths):
-                got[k] = room[:, at : at + width]
-                at = at + width
+            for i, width in enumerate(widths):
+                place[first + i] = (room, sum(widths[:i]), width)
 
-        def fetch(u, d):
-            t, v0, v1 = units[u]
-            n = v1 - v0
-            gather(got[2 * u + d // 2][:, (d % 2) * n : (d % 2 + 1) * n], t, d, v0, v1)
+        def got(u, d, count):
+            room, at, width = place[LISTS * u + d]
+            return room[:, at : at + count * width]
+
+        def gather(u, d):
+            t, v0, v1 = UNITS[u]
+            nc.vector.tensor_copy(got(u, d, 1), h[t][:].indirect(lists[d][:, v0 // ENTRIES : v1 // ENTRIES]))
 
         def step(u):
-            t, v0, v1 = units[u]
+            t, v0, v1 = UNITS[u]
             n = v1 - v0
-            fetch(u, 2)
-            fetch(u, 3)
-            fetch(u + 1, 0)
+            gather(u, 2)
+            gather(u, 3)
+            gather(u + 1, 0)
             pair = tile([P, 2 * n], BF16, "pair%d" % u)
-            nc.vector.tensor_tensor(pair[:], got[2 * u], got[2 * u + 1], MAX)
-            fetch(u + 1, 1)
+            nc.vector.tensor_tensor(pair[:], got(u, 0, 2), got(u, 2, 2), MAX)
+            gather(u + 1, 1)
             for part, a, b, base in z_parts(v0, v1):
                 nc.vector.tensor_tensor(
                     part[:, t, a - base : b - base], pair[:, a - v0 : b - v0], pair[:, n + a - v0 : n + b - v0], MAX
                 )
 
-        stage(0, 5, None)
-        fetch(0, 0)
-        fetch(0, 1)
+        make_room(0, 6, None)
+        gather(0, 0)
+        gather(0, 1)
         step(0)
+        quantize(w23_code[:], w23_scale[:], w23_woven[:])
+        make_room(6, 10, "raw1")
         step(1)
-        quantize(w23_codes, w23_scales, w23_bf, 0, 2 * N)
-        stage(5, 7, "raw1")
+        quantize_h(0)
+        open_groups(0)
+        make_room(10, 14, "h_planes0")
         step(2)
-        quantize(h_codes[:, 0:HALF], h_scales[:, 0:HALF], h_woven[0], 0, HALF)
-        own_products(0)
-        stage(7, 9, "h_bf0")
+        quantize_h(1)
+        for chunk in range(1, len(CHUNKS)):
+            open_groups(chunk)
+        make_room(14, 22, "h_planes1")
         step(3)
-        quantize(h_codes[:, HALF:T], h_scales[:, HALF:T], h_woven[1], 0, HALF)
-        for index in range(1, 4):
-            own_products(index)
-        stage(9, 13, "h_bf1")
-        step(4)
         woven0 = weave_z(0, nc.scalar.copy)
+        step(4)
+        close_groups(0, woven0)
+        store(0, 0)
+        make_room(22, 26, "z0")
+        make_room(26, 31, "h_planes1")
         step(5)
-        finish(0, woven0)
-        stage(13, 19, "z0")
-        step(6)
-        step(7)
         woven1 = weave_z(1, nc.scalar.copy)
-        step(8)
+        step(6)
         woven2 = weave_z(2, nc.scalar.copy)
+        store(0, 1)
 
-        v0, v1 = chunks[3]
-        n = v1 - v0
-        two = tile([P, n], BF16, "last_two")
-        nc.vector.tensor_tensor(two[:], got[18][:, 0:n], got[18][:, n : 2 * n], MAX)
-        finish(1, woven1)
-        stage(19, 20, "z1")
-        fetch(9, 2)
-        fetch(9, 3)
-        three = tile([P, n], BF16, "last_three")
-        nc.vector.tensor_tensor(three[:], two[:], got[19][:, 0:n], MAX)
-        finish(2, woven2)
-        nc.vector.tensor_tensor(z[2][:, 3, n : 2 * n], three[:], got[19][:, n : 2 * n], MAX)
-        finish(3, weave_z(3, nc.vector.tensor_copy))
+        last_unit = len(UNITS) - 1
+        t, v0, v1 = UNITS[last_unit]
+        ((part, a, b, base),) = z_parts(v0, v1)
+        gather(last_unit, 2)
+        of_two = tile([P, v1 - v0], BF16, "of_two")
+        nc.vector.tensor_tensor(of_two[:], got(last_unit, 0, 1), got(last_unit, 1, 1), MAX)
+        of_three = tile([P, v1 - v0], BF16, "of_three")
+        nc.vector.tensor_tensor(of_three[:], of_two[:], got(last_unit, 2, 1), MAX)
+        close_groups(1, woven1)
+        store(1, 0)
+        store(1, 1)
+        make_room(31, 32, "z1")
+        gather(last_unit, 3)
+        close_groups(2, woven2)
+        store(2, 0)
+        store(2, 1)
+        nc.vector.tensor_tensor(part[:, t, a - base : b - base], of_three[:], got(last_unit, 3, 1), MAX)
+        close_groups(LAST, weave_z(LAST, nc.vector.tensor_copy))
+        store(LAST, 0)
+        store(LAST, 1)

@@ -70,10 +70,10 @@ def tile_picked_wsagecat_maxrelu_l_kernel(
 
         load_w1(0, 0)
         load_w1(0, 1)
-        for q in range(4):
+        for r in range(4):
             nc.sync.dma_start(
-                out=x_scale[32 * q : 32 * q + 4, :, :].bitcast(I32),
-                in_=x_scales[:, 4 * q : 4 * q + 4, :].rearrange("g r c -> r g c").bitcast(I32),
+                out=x_scale[r:P:32, :, :].bitcast(I32),
+                in_=x_scales[:, r:16:4, :].rearrange("g q c -> q g c").bitcast(I32),
             )
         x_code = [tile([P, 2 * T], U8, "x_code%d" % g) for g in range(2)]
         nc.sync.dma_start(out=x_code[0][:].bitcast(I32), in_=x_words[0].bitcast(I32))

from contextlib import ExitStack

import concourse.mybir as mybir

K, T, H, N = 1024, 1024, 512, 256
FLOPS = 2 * K * H * T + 2 * 2 * H * N * T

F32 = mybir.dt.float32
BF16 = mybir.dt.bfloat16
I32 = mybir.dt.int32
U32 = mybir.dt.uint32
U16 = mybir.dt.uint16
U8 = mybir.dt.uint8
FP8X4 = mybir.dt.float8_e4m3fn_x4
FP4X4 = mybir.dt.float4_e2m1fn_x4
MAX = mybir.AluOpType.max
RELU = mybir.ActivationFunctionType.Relu

P = 128
PACK = 4
K_PASS = P * PACK
BANK = 512
BANKS = 8
LISTS = 4
ENTRIES = 16
RUN = 4

VECTOR_DEALS = 80

CHUNKS = ((0, 512), (512, 768), (768, 896), (896, 1024))
LAST = len(CHUNKS) - 1
Z_TILES = ((0, 512), (512, 768), (768, 1024))
UNITS = ((0, 0, T), (1, 0, T), (2, 0, 512), (3, 0, 512), (2, 512, T)) + tuple((3, a, b) for a, b in CHUNKS[1:])
WHOLE_PLANES = 2


def tile_picked_wsagecat_maxrelu_l_kernel(
    tc, x_words, x_scales, w1, w2, w3, pos1, pos2, pos3, pos4, out
):
    nc = tc.nc
    with ExitStack() as ctx:
        held = ctx.enter_context(tc.tile_pool(name="held", bufs=1))
        sb = ctx.enter_context(tc.tile_pool(name="sb", bufs=1))
        psum = ctx.enter_context(tc.psum_pool(name="psum", bufs=1))

        def tile(shape, dtype, name, tag=None):
            return sb.tile(shape, dtype, name=name, tag=tag or name, align_bytes=64)

        def bank(number, width, name):
            return psum.tile([P, width], F32, name=name, tag="bank%d" % number)

        def quantize(codes, scales, values):
            nc.vector.quantize_mx(out=codes.bitcast(FP8X4), scales=scales, in_=values)

        def weave(copy, dst, planes):
            copy(
                out=dst.rearrange("p (c i t) -> p c t i", i=RUN, t=PACK),
                in_=planes.rearrange("p t (c i) -> p c t i", i=RUN),
            )

        x_scale = tile([P, 2, T], U8, "x_scale")
        nc.gpsimd.memset(x_scale[:].bitcast(I32), 0)

        w1_raw = {}

        def load_w1(g, u):
            w1_raw[g, u] = tile([P, 2, H], F32, "w1_raw%d_%d" % (g, u), "raw%d" % u if g == 0 else None)
            rows = w1[g * K_PASS : (g + 1) * K_PASS, :].rearrange("(p j) c -> p j c", j=PACK)
            nc.sync.dma_start(out=w1_raw[g, u][:], in_=rows[:, 2 * u : 2 * u + 2, :])

        load_w1(0, 0)
        load_w1(0, 1)
        for r in range(4):
            nc.sync.dma_start(
                out=x_scale[r:P:32, :, :].bitcast(I32),
                in_=x_scales[:, r:16:4, :].rearrange("g q c -> q g c").bitcast(I32),
            )
        x_code = [tile([P, 2 * T], U8, "x_code%d" % g) for g in range(2)]
        nc.sync.dma_start(out=x_code[0][:].bitcast(I32), in_=x_words[0].bitcast(I32))
        load_w1(1, 0)
        load_w1(1, 1)
        nc.sync.dma_start(out=x_code[1][:].bitcast(I32), in_=x_words[1].bitcast(I32))
        lists = []
        for d, pos in enumerate((pos1, pos2, pos3, pos4)):
            offsets = held.tile([P, T // ENTRIES], U16, name="list%d" % d)
            nc.sync.dma_start(offsets[:], pos)
            lists.append(offsets)

        w1_code = [tile([P, H], U32, "w1_code%d" % g) for g in range(2)]
        w1_scale = [tile([P, H], U8, "w1_scale%d" % g) for g in range(2)]
        w1_dealt = [tile([P, PACK * H], BF16, "w1_dealt%d" % g) for g in range(2)]

        def deal_views(g, u):
            dst = w1_dealt[g][:].rearrange("p (t m j) -> p m j t", t=PACK, j=PACK)[:, :, 2 * u : 2 * u + 2]
            src = w1_raw[g, u][:].rearrange("p j (m t) -> p m j t", t=PACK)
            return dst, src

        def deal(g, u):
            dst, src = deal_views(g, u)
            nc.vector.tensor_copy(out=dst[:, 0:VECTOR_DEALS], in_=src[:, 0:VECTOR_DEALS])
            nc.scalar.copy(out=dst[:, VECTOR_DEALS:P], in_=src[:, VECTOR_DEALS:P])

        def quantize_w1(g, t0, t1):
            cols = slice(t0 * P, t1 * P)
            quantize(w1_code[g][:, cols], w1_scale[g][:, cols], w1_dealt[g][:, t0 * K_PASS : t1 * K_PASS])

        deal(0, 0)
        deal(0, 1)
        quantize_w1(0, 0, 1)
        quantize_w1(0, 1, 2)
        quantize_w1(0, 2, 4)
        deal(1, 0)
        dst, src = deal_views(1, 1)
        nc.vector.tensor_copy(out=dst[:, :, :, 0], in_=src[:, :, :, 0])
        nc.scalar.copy(out=dst[:, :, :, 1:3], in_=src[:, :, :, 1:3])
        quantize_w1(1, 0, 1)
        nc.vector.tensor_copy(out=dst[:, :, :, 3], in_=src[:, :, :, 3])
        quantize_w1(1, 1, 2)
        quantize_w1(1, 2, 4)

        w23_raw = []
        for e, w in enumerate((w2, w3)):
            raw = tile([P, PACK, N], F32, "w23_raw%d" % e, "raw%d" % e)
            nc.sync.dma_start(out=raw[:], in_=w.rearrange("(p j) n -> p j n", j=PACK))
            w23_raw.append(raw)

        h = [tile([P, 2 * T if t < WHOLE_PLANES else T], F32, "h%d" % t) for t in range(PACK)]
        for t in range(PACK):
            acc = [bank(2 * (t % 2) + c, BANK, "acc%d_%d" % (t, c)) for c in range(2)]
            for g in range(2):
                for c in range(2):
                    nc.tensor.matmul_mx(
                        out=acc[c][:],
                        lhsT=w1_code[g][:, t * P : (t + 1) * P].bitcast(FP8X4),
                        lhsT_scale=w1_scale[g][:, t * P : (t + 1) * P],
                        rhs=x_code[g][:, 2 * c * BANK : 2 * (c + 1) * BANK].bitcast(FP4X4),
                        rhs_scale=x_scale[:, g, c * BANK : (c + 1) * BANK],
                        start=(g == 0),
                        stop=(g == 1),
                    )
            nc.scalar.activation(h[t][:, 0:BANK], acc[0][:], RELU)
            if t == 0:
                nc.vector.tensor_scalar_max(h[t][:, BANK:T], acc[1][:], 0.0)
            else:
                nc.scalar.activation(h[t][:, BANK:T], acc[1][:], RELU)

        w23_woven = tile([P, 2 * N * PACK], BF16, "w23_woven")
        for e in range(2):
            weave(nc.scalar.copy, w23_woven[:, e * N * PACK : (e + 1) * N * PACK], w23_raw[e][:])
        w23_code = tile([P, 2 * N], U32, "w23_code")
        w23_scale = tile([P, 2 * N], U8, "w23_scale")

        h_woven = []
        for c in range(2):
            planes = tile([P, PACK, BANK], BF16, "h_planes%d" % c)
            for t in range(PACK):
                nc.scalar.copy(planes[:, t, :], h[t][:, c * BANK : (c + 1) * BANK])
            woven = tile([P, PACK * BANK], BF16, "h_woven%d" % c)
            weave(nc.scalar.copy, woven[:], planes[:])
            h_woven.append(woven)
        h_code = tile([P, T], U32, "h_code")
        h_scale = tile([P, T], U8, "h_scale")

        def quantize_h(c):
            cols = slice(c * BANK, (c + 1) * BANK)
            quantize(h_code[:, cols], h_scale[:, cols], h_woven[c][:])

        z = [tile([P, PACK, b - a], BF16, "z%d" % c) for c, (a, b) in enumerate(Z_TILES)]
        res = {}

        def z_parts(v0, v1):
            return [(z[c], max(v0, a), min(v1, b), a) for c, (a, b) in enumerate(Z_TILES) if max(v0, a) < min(v1, b)]

        def multiply(chunk, m, e, codes, scales):
            cols = slice(e * N + m * P, e * N + (m + 1) * P)
            nc.tensor.matmul_mx(
                out=res[chunk, m][:],
                lhsT=w23_code[:, cols].bitcast(FP8X4),
                lhsT_scale=w23_scale[:, cols],
                rhs=codes.bitcast(FP8X4),
                rhs_scale=scales,
                start=(e == 0),
                stop=(e == 1),
            )

        def open_groups(chunk):
            v0, v1 = CHUNKS[chunk]
            for m in range(2):
                res[chunk, m] = bank((4 + 2 * chunk + m) % BANKS, v1 - v0, "res%d_%d" % (chunk, m))
                multiply(chunk, m, 0, h_code[:, v0:v1], h_scale[:, v0:v1])

        def weave_z(chunk, copy):
            v0, v1 = CHUNKS[chunk]
            ((part, a, b, base),) = z_parts(v0, v1)
            woven = tile([P, PACK * (v1 - v0)], BF16, "z_woven%d" % chunk)
            weave(copy, woven[:], part[:, :, a - base : b - base])
            return woven

        def close_groups(chunk, woven):
            v0, v1 = CHUNKS[chunk]
            codes = tile([P, v1 - v0], U32, "z_code%d" % chunk)
            scales = tile([P, v1 - v0], U8, "z_scale%d" % chunk)
            quantize(codes[:], scales[:], woven[:])
            for m in range(2):
                multiply(chunk, m, 1, codes[:], scales[:])

        def store(chunk, m):
            v0, v1 = CHUNKS[chunk]
            result = tile([P, v1 - v0], F32, "result%d_%d" % (chunk, m))
            if (chunk, m) == (LAST, 1):
                nc.vector.tensor_scalar_max(result[:], res[chunk, m][:], 0.0)
            else:
                nc.scalar.activation(result[:], res[chunk, m][:], RELU)
            queue = nc.scalar if (chunk, m) == (LAST, 0) else nc.sync
            queue.dma_start(out=out[m * P : (m + 1) * P, v0:v1], in_=result[:])

        place = {}

        def make_room(first, end, tag):
            widths = [UNITS[k // LISTS][2] - UNITS[k // LISTS][1] for k in range(first, end)]
            room = tile([P, sum(widths)], BF16, "got%d" % first, tag)
            for i, width in enumerate(widths):
                place[first + i] = (room, sum(widths[:i]), width)

        def got(u, d, count):
            room, at, width = place[LISTS * u + d]
            return room[:, at : at + count * width]

        def gather(u, d):
            t, v0, v1 = UNITS[u]
            nc.vector.tensor_copy(got(u, d, 1), h[t][:].indirect(lists[d][:, v0 // ENTRIES : v1 // ENTRIES]))

        def step(u):
            t, v0, v1 = UNITS[u]
            n = v1 - v0
            gather(u, 2)
            gather(u, 3)
            gather(u + 1, 0)
            pair = tile([P, 2 * n], BF16, "pair%d" % u)
            nc.vector.tensor_tensor(pair[:], got(u, 0, 2), got(u, 2, 2), MAX)
            gather(u + 1, 1)
            for part, a, b, base in z_parts(v0, v1):
                nc.vector.tensor_tensor(
                    part[:, t, a - base : b - base], pair[:, a - v0 : b - v0], pair[:, n + a - v0 : n + b - v0], MAX
                )

        make_room(0, 6, None)
        gather(0, 0)
        gather(0, 1)
        step(0)
        quantize(w23_code[:], w23_scale[:], w23_woven[:])
        make_room(6, 10, "raw1")
        step(1)
        quantize_h(0)
        open_groups(0)
        make_room(10, 14, "h_planes0")
        step(2)
        quantize_h(1)
        for chunk in range(1, len(CHUNKS)):
            open_groups(chunk)
        make_room(14, 22, "h_planes1")
        step(3)
        woven0 = weave_z(0, nc.scalar.copy)
        step(4)
        close_groups(0, woven0)
        store(0, 0)
        make_room(22, 26, "z0")
        make_room(26, 31, "h_planes1")
        step(5)
        woven1 = weave_z(1, nc.scalar.copy)
        step(6)
        woven2 = weave_z(2, nc.scalar.copy)
        store(0, 1)

        last_unit = len(UNITS) - 1
        t, v0, v1 = UNITS[last_unit]
        ((part, a, b, base),) = z_parts(v0, v1)
        gather(last_unit, 2)
        of_two = tile([P, v1 - v0], BF16, "of_two")
        nc.vector.tensor_tensor(of_two[:], got(last_unit, 0, 1), got(last_unit, 1, 1), MAX)
        of_three = tile([P, v1 - v0], BF16, "of_three")
        nc.vector.tensor_tensor(of_three[:], of_two[:], got(last_unit, 2, 1), MAX)
        close_groups(1, woven1)
        store(1, 0)
        store(1, 1)
        make_room(31, 32, "z1")
        gather(last_unit, 3)
        close_groups(2, woven2)
        store(2, 0)
        store(2, 1)
        nc.vector.tensor_tensor(part[:, t, a - base : b - base], of_three[:], got(last_unit, 3, 1), MAX)
        close_groups(LAST, weave_z(LAST, nc.vector.tensor_copy))
        store(LAST, 0)
        store(LAST, 1)
